import numpy as np
import ml_dtypes


def mxq(x, axis, fmt="e4m3"):
    dtype, down = {"e4m3": (ml_dtypes.float8_e4m3fn, 7), "e5m2": (ml_dtypes.float8_e5m2, 14)}[fmt]
    v = np.moveaxis(np.asarray(x, np.float32).astype(ml_dtypes.bfloat16).astype(np.float64), axis, -1)
    blocks = v.reshape(v.shape[:-1] + (-1, 32))
    amax = np.abs(blocks).max(-1, keepdims=True)
    byte = np.maximum(np.where(amax > 0, np.frexp(amax)[1] - 1 + 127, 0) - down, 1)
    scale = np.exp2(byte - 127.0)
    codes = (blocks / scale).astype(np.float32).astype(dtype).astype(np.float64)
    return np.moveaxis((codes * scale).reshape(v.shape), -1, axis)


WIDE = False


def mx_kscale(k):
    if not WIDE:
        return np.ones(k)
    levels = np.array([10, -10, 5, -5, 0])
    if k % 512:
        return np.exp2(np.random.permutation(np.resize(levels, k // 32))).repeat(32)
    a = np.empty((k // 512, 16))
    for p in range(k // 512):
        a[p, :8] = np.random.permutation(np.resize(levels, 8))
        for g in range(8):
            far = levels[np.abs(levels - a[p, g]) >= 10]
            a[p, g + 8] = far[np.random.randint(len(far))]
    return np.exp2(a.ravel()).repeat(32)


def f64(x):
    return np.asarray(x).astype(np.float64)


def striped8(idx):
    return np.asarray(idx).reshape(8, -1, 16).transpose(0, 2, 1).reshape(128, -1).astype(np.uint16)


def unstriped8(offs):
    return offs.reshape(8, 16, -1).transpose(0, 2, 1).reshape(8, -1).astype(np.int64)


def pick8(x, idx, run):
    r = np.arange(len(x))
    return x[r[:, None], idx[r % (8 * run) // run]]


E2M1 = np.array([0.0, 0.5, 1.0, 1.5, 2.0, 3.0, 4.0, 6.0, -0.0, -0.5, -1.0, -1.5, -2.0, -3.0, -4.0, -6.0])


def pack_weight(w, fmt):
    k, n = w.shape
    w = f64(np.asarray(w, np.float32).astype(ml_dtypes.bfloat16)).reshape(k // 32, 32, n)
    amax = np.abs(w).max(1)
    if fmt == "e4m3":
        byte = np.frexp(amax)[1] - 1 + 127 - 7
    else:
        mant, ex = np.frexp(amax / 6.0)
        byte = np.where(mant > 0.5, ex, ex - 1) + 127
    byte = np.clip(np.where(amax > 0, byte, 1), 1, 254)
    scaled = (w * np.exp2(127.0 - byte)[:, None, :]).reshape(k, n).astype(np.float32)
    by_word = np.ascontiguousarray(scaled.reshape(k // 512, 128, 4, n).transpose(0, 1, 3, 2))
    if fmt == "e4m3":
        words = by_word.astype(ml_dtypes.float8_e4m3fn).view(np.uint8)
    else:
        c = by_word.astype(ml_dtypes.float4_e2m1fn).view(np.uint8) & 0xF
        words = (c[..., 0::2] | (c[..., 1::2] << 4)).reshape(k // 512, 128, 2 * n)
    return np.ascontiguousarray(words), np.ascontiguousarray(byte.astype(np.uint8).reshape(k // 512, 16, n))


def unpack_weight(words, scales, fmt):
    g, _, n = scales.shape
    words = np.ascontiguousarray(words).reshape(g, 128, n, -1)
    if fmt == "e4m3":
        vals = words.view(ml_dtypes.float8_e4m3fn).astype(np.float64)
    else:
        nib = np.empty((g, 128, n, 4), np.uint8)
        nib[..., 0::2] = words & 0xF
        nib[..., 1::2] = words >> 4
        vals = E2M1[nib]
    vals = vals * np.repeat(np.exp2(scales.astype(np.float64) - 127.0), 8, axis=1)[..., None]
    return vals.transpose(0, 1, 3, 2).reshape(g * 512, n)


def bf(x):
    return np.asarray(x, np.float32).astype(ml_dtypes.bfloat16)


def planes(Y):
    r, m = Y.shape
    b = f64(bf(Y)).reshape(r // 32, 32, m)
    amax = np.abs(b).max(1)
    byte = np.clip(np.where(amax > 0, np.frexp(amax)[1] - 1 + 127 - 7, 1), 1, 254)
    codes = (b * np.exp2(127.0 - byte)[:, None, :]).reshape(r, m).astype(np.float32).astype(ml_dtypes.float8_e4m3fn).view(np.uint8)
    words = codes.reshape(r // 512, 128, 4, m).transpose(0, 1, 3, 2)
    return np.ascontiguousarray(words), np.ascontiguousarray(byte.astype(np.uint8).reshape(r // 512, 16, m))


K, T, J, N, L = 512, 1024, 256, 512, 512


def setup_inputs():
    n = np.random.standard_normal
    idx = np.stack([np.random.permutation(T)[:J] for _ in range(8)])
    fk = mx_kscale(K)
    fl = mx_kscale(L)
    xtp = pack_weight(n((K, T)) / fk[:, None], "e2m1")
    sxp = pack_weight(n((L, J)) / fl[:, None], "e4m3")
    wsp = pack_weight(n((L, N)) * 1 / np.sqrt(L) * fl[:, None], "e2m1")
    return {
        "xt_words": xtp[0],
        "xt_scales": xtp[1],
        "w": (n((K, N)) * 1 / np.sqrt(K) * fk[:, None]).astype(np.float32),
        "sx_words": sxp[0],
        "sx_scales": sxp[1],
        "ws_words": wsp[0],
        "ws_scales": wsp[1],
        "offs": striped8(idx),
    }


def reference(xt_words, xt_scales, w, sx_words, sx_scales, ws_words, ws_scales, offs):
    idx = unstriped8(offs)
    xtu = unpack_weight(xt_words, xt_scales, "e2m1")
    sxu = unpack_weight(sx_words, sx_scales, "e4m3")
    wsu = unpack_weight(ws_words, ws_scales, "e2m1")
    wq = mxq(f64(w), 0, "e4m3")
    z = wq.T @ xtu
    p = wsu.T @ sxu
    pt = np.tanh(p)
    pg = np.zeros((N, T))
    pg[np.arange(N)[:, None], idx[np.arange(N) % 512 // 64]] = pt
    y = z + pg
    words, scales = planes(y)
    return y, words, scales

from contextlib import ExitStack

import concourse.mybir as mybir

K, T, J, N, L = 512, 1024, 256, 512, 512
FLOPS = 2 * K * N * T + 2 * L * N * J

F32 = mybir.dt.float32
BF16 = mybir.dt.bfloat16
I32 = mybir.dt.int32
U32 = mybir.dt.uint32
U16 = mybir.dt.uint16
U8 = mybir.dt.uint8
FP8X4 = mybir.dt.float8_e4m3fn_x4
FP4X4 = mybir.dt.float4_e2m1fn_x4
ADD = mybir.AluOpType.add
TANH = mybir.ActivationFunctionType.Tanh

P = 128
PACK = 4
BANK = 512
CHUNK = 256


def load_scales(queues, plane, scales):
    for q in range(4):
        queues[q % 2].dma_start(
            out=plane[32 * q : 32 * q + 4, :].bitcast(I32), in_=scales[0, 4 * q : 4 * q + 4, :].bitcast(I32)
        )


def tile_list_head_scatter_on_shared_pl_kernel(
    tc, xt_words, xt_scales, w, sx_words, sx_scales, ws_words, ws_scales, offs, out_0, out_1, out_2
):
    nc = tc.nc
    with ExitStack() as ctx:
        keep = ctx.enter_context(tc.tile_pool(name="keep", bufs=1))
        psum = ctx.enter_context(tc.psum_pool(name="psum", bufs=1))

        offsets = keep.tile([P, J // 16], U16, name="offsets")
        ws_raw = keep.tile([P, 2 * N], U8, name="ws_raw", align_bytes=64)
        ws_sraw = keep.tile([P, N], U8, name="ws_sraw", align_bytes=64)
        sx_c = keep.tile([P, J], U32, name="sx_c", align_bytes=64)
        sx_s = keep.tile([P, J], U8, name="sx_s", align_bytes=64)
        xt_s = keep.tile([P, T], U8, name="xt_s", align_bytes=64)

        for plane in (ws_sraw, sx_s, xt_s):
            nc.vector.memset(plane[:].bitcast(I32), 0)
        warm_in = keep.tile([P, 1], F32, name="warm_in", tag="xt_c", align_bytes=64)
        warm_out = keep.tile([P, 1], F32, name="warm_out", tag="w_raw", align_bytes=64)
        nc.vector.memset(warm_in[:], 0.0)
        nc.scalar.activation(warm_out[:], warm_in[:], TANH)
        xt_c = keep.tile([P, 2 * T], U8, name="xt_c", tag="xt_c", align_bytes=64)
        w_raw = keep.tile([P, PACK * N], F32, name="w_raw", tag="w_raw", align_bytes=64)

        both = (nc.sync, nc.sync)
        nc.sync.dma_start(out=ws_raw[:].bitcast(I32), in_=ws_words[0].bitcast(I32))
        nc.sync.dma_start(out=sx_c[:].bitcast(I32), in_=sx_words[0].rearrange("p c r -> p (c r)").bitcast(I32))
        load_scales(both, ws_sraw, ws_scales)
        load_scales(both, sx_s, sx_scales)
        nc.sync.dma_start(offsets[:], offs)
        nc.sync.dma_start(out=w_raw[:], in_=w.rearrange("(p j) n -> p (j n)", j=PACK))
        nc.sync.dma_start(out=xt_c[:].bitcast(I32), in_=xt_words[0].bitcast(I32))
        load_scales(both, xt_s, xt_scales)

        banks = {}
        p_ps = []
        for t in range(PACK):
            ws_c = keep.tile([P, 2 * P], U8, name=f"ws_c{t}", align_bytes=64)
            ws_s = keep.tile([P, P], U8, name=f"ws_s{t}", align_bytes=64)
            nc.vector.tensor_copy(
                out=ws_c[:].rearrange("p (m b) -> p m b", b=2),
                in_=ws_raw[:].rearrange("p (m t b) -> p t m b", t=PACK, b=2)[:, t],
            )
            nc.vector.tensor_copy(out=ws_s[:], in_=ws_sraw[:].rearrange("p (m t) -> p t m", t=PACK)[:, t])
            acc = psum.tile([P, J], F32, name=f"p_ps{t}", tag=f"bank{t + 4}")
            nc.tensor.matmul_mx(
                out=acc[:], lhsT=ws_c[:].bitcast(FP4X4), lhsT_scale=ws_s[:],
                rhs=sx_c[:].bitcast(FP8X4), rhs_scale=sx_s[:], start=True, stop=True,
            )
            p_ps.append(acc)

        pg = [keep.tile([P, T], F32, name=f"pg{t}") for t in range(PACK)]
        for t in range(PACK):
            nc.vector.memset(pg[t][:].bitcast(I32), 0)

        def tanh_and_scatter(t, tag):
            pt = keep.tile([P, J], F32, name=f"pt{t}", tag=tag, align_bytes=64)
            nc.scalar.activation(pt[:], p_ps[t][:], TANH)
            nc.vector.tensor_copy(pg[t][:].indirect(offsets[:]), pt[:])

        for t in range(PACK - 1):
            tanh_and_scatter(t, f"pt{t}")

        w_bf = keep.tile([P, PACK * N], BF16, name="w_bf", align_bytes=64)
        nc.scalar.copy(
            out=w_bf[:].rearrange("p (t m j) -> p m t j", t=PACK, j=PACK),
            in_=w_raw[:].rearrange("p (j m t) -> p m t j", t=PACK, j=PACK),
        )
        w_c = keep.tile([P, N], U32, name="w_c", align_bytes=64)
        w_s = keep.tile([P, N], U8, name="w_s", align_bytes=64)
        nc.vector.quantize_mx(out=w_c[:].bitcast(FP8X4), scales=w_s[:], in_=w_bf[:])

        tanh_and_scatter(PACK - 1, "w_raw")

        for h in range(T // BANK):
            for t in range(PACK):
                acc = psum.tile([P, BANK], F32, name=f"z_ps{h}{t}", tag=f"bank{4 * h + t}")
                nc.tensor.matmul_mx(
                    out=acc[:], lhsT=w_c[:, t * P : (t + 1) * P].bitcast(FP8X4), lhsT_scale=w_s[:, t * P : (t + 1) * P],
                    rhs=xt_c[:, 2 * h * BANK : 2 * (h + 1) * BANK].bitcast(FP4X4), rhs_scale=xt_s[:, h * BANK : (h + 1) * BANK],
                    start=True, stop=True,
                )
                banks[(h, t)] = acc

        y_s = keep.tile([P, T], U8, name="y_s", align_bytes=64)
        out_rows = out_0.rearrange("(p t) c -> p t c", t=PACK)
        out_words = out_1[0].rearrange("p c r -> p (c r)").bitcast(I32)
        y_bf = {}

        def add_and_round(c):
            c0 = c * CHUNK
            h, b0 = divmod(c0, BANK)
            y = keep.tile([P, PACK, CHUNK], F32, name=f"y{c}")
            for t in range(PACK):
                nc.vector.tensor_tensor(y[:, t, :], banks[(h, t)][:, b0 : b0 + CHUNK], pg[t][:, c0 : c0 + CHUNK], ADD)
            nc.sync.dma_start(out=out_rows[:, :, c0 : c0 + CHUNK], in_=y[:])
            y_bf[c] = keep.tile([P, PACK * CHUNK], BF16, name=f"y_bf{c}", align_bytes=64)
            nc.scalar.copy(
                out=y_bf[c][:].rearrange("p (c i t) -> p c t i", t=PACK, i=4),
                in_=y[:].rearrange("p t (c i) -> p c t i", i=4),
            )

        def quantize(c):
            c0 = c * CHUNK
            y_c = keep.tile([P, CHUNK], U32, name=f"y_c{c}", align_bytes=64)
            nc.vector.quantize_mx(out=y_c[:].bitcast(FP8X4), scales=y_s[:, c0 : c0 + CHUNK], in_=y_bf[c][:])
            nc.sync.dma_start(out=out_words[:, c0 : c0 + CHUNK], in_=y_c[:].bitcast(I32))

        chunks = T // CHUNK
        for c in range(chunks):
            add_and_round(c)
            if c >= 1:
                quantize(c - 1)
        quantize(chunks - 1)
        for q in range(4):
            queue = nc.sync if q % 2 == 0 else nc.scalar
            queue.dma_start(out=out_2[0, 4 * q : 4 * q + 4, :].bitcast(I32), in_=y_s[32 * q : 32 * q + 4, :].bitcast(I32))
